import numpy as np
import ml_dtypes


def mxq(x, axis, fmt="e4m3"):
    dtype, down = {"e4m3": (ml_dtypes.float8_e4m3fn, 7), "e5m2": (ml_dtypes.float8_e5m2, 14)}[fmt]
    v = np.moveaxis(np.asarray(x, np.float32).astype(ml_dtypes.bfloat16).astype(np.float64), axis, -1)
    blocks = v.reshape(v.shape[:-1] + (-1, 32))
    amax = np.abs(blocks).max(-1, keepdims=True)
    byte = np.maximum(np.where(amax > 0, np.frexp(amax)[1] - 1 + 127, 0) - down, 1)
    scale = np.exp2(byte - 127.0)
    codes = (blocks / scale).astype(np.float32).astype(dtype).astype(np.float64)
    return np.moveaxis((codes * scale).reshape(v.shape), -1, axis)


WIDE = False


def mx_kscale(k):
    if not WIDE:
        return np.ones(k)
    levels = np.array([10, -10, 5, -5, 0])
    if k % 512:
        return np.exp2(np.random.permutation(np.resize(levels, k // 32))).repeat(32)
    a = np.empty((k // 512, 16))
    for p in range(k // 512):
        a[p, :8] = np.random.permutation(np.resize(levels, 8))
        for g in range(8):
            far = levels[np.abs(levels - a[p, g]) >= 10]
            a[p, g + 8] = far[np.random.randint(len(far))]
    return np.exp2(a.ravel()).repeat(32)


BF16 = ml_dtypes.bfloat16


def bf(x):
    return np.asarray(x, np.float32).astype(BF16)


def f64(x):
    return np.asarray(x).astype(np.float64)


E2M1 = np.array([0.0, 0.5, 1.0, 1.5, 2.0, 3.0, 4.0, 6.0, -0.0, -0.5, -1.0, -1.5, -2.0, -3.0, -4.0, -6.0])


def pack_weight(w, fmt):
    k, n = w.shape
    w = f64(bf(w)).reshape(k // 32, 32, n)
    amax = np.abs(w).max(1)
    if fmt == "e4m3":
        byte = np.frexp(amax)[1] - 1 + 127 - 7
    else:
        mant, ex = np.frexp(amax / 6.0)
        byte = np.where(mant > 0.5, ex, ex - 1) + 127
    byte = np.clip(np.where(amax > 0, byte, 1), 1, 254)
    scaled = (w * np.exp2(127.0 - byte)[:, None, :]).reshape(k, n).astype(np.float32)
    by_word = np.ascontiguousarray(scaled.reshape(k // 512, 128, 4, n).transpose(0, 1, 3, 2))
    if fmt == "e4m3":
        words = by_word.astype(ml_dtypes.float8_e4m3fn).view(np.uint8)
    else:
        c = by_word.astype(ml_dtypes.float4_e2m1fn).view(np.uint8) & 0xF
        words = c[..., 0::2] | (c[..., 1::2] << 4)
    return np.ascontiguousarray(words), np.ascontiguousarray(byte.astype(np.uint8).reshape(k // 512, 16, n))


def unpack_weight(words, scales, fmt):
    g, p, n, _ = words.shape
    if fmt == "e4m3":
        vals = np.ascontiguousarray(words).view(ml_dtypes.float8_e4m3fn).astype(np.float64)
    else:
        nib = np.empty((g, p, n, 4), np.uint8)
        nib[..., 0::2] = words & 0xF
        nib[..., 1::2] = words >> 4
        vals = E2M1[nib]
    vals = vals * np.repeat(np.exp2(scales.astype(np.float64) - 127.0), 8, axis=1)[..., None]
    return vals.transpose(0, 1, 3, 2).reshape(g * 512, n)
def pack4(w):
    words, scales = pack_weight(w, "e2m1")
    return words.reshape(words.shape[0], 128, -1), scales


def unpack4(words, scales):
    return unpack_weight(words.reshape(words.shape[0], 128, -1, 2), scales, "e2m1")


M, K, N, R, T = 1024, 1024, 1024, 512, 2


def setup_inputs():
    s, r = mx_kscale(K), mx_kscale(R)
    x = bf(np.random.standard_normal((M, K)) / np.sqrt(K) * s)
    w_words, w_scales = pack_weight(np.random.standard_normal((K, N)) / s[:, None], "e4m3")
    u_words, u_scales = pack4(np.random.standard_normal((R, T * K)) * r[:, None] / np.tile(s, T))
    v_words, v_scales = pack4(np.random.standard_normal((R, T * N)) / np.sqrt(R) / r[:, None])
    return {"x": x,
            "w_words": w_words, "w_scales": w_scales,
            "u_words": u_words, "u_scales": u_scales,
            "v_words": v_words, "v_scales": v_scales,
            "lim": bf(np.random.uniform(0.5, 1.5, (T, K)) / s),
            "lam": bf(np.random.uniform(0.3, 1.0, (M, T)))}


def reference(x, w_words, w_scales, u_words, u_scales, v_words, v_scales, lim, lam):
    w = unpack_weight(w_words, w_scales, "e4m3")
    u = unpack4(u_words, u_scales)
    v = unpack4(v_words, v_scales)
    lim, lam = f64(lim), f64(lam)
    xq = mxq(f64(x), 1, "e4m3")
    y = xq @ w
    for i in range(T):
        d = u[:, i * K:(i + 1) * K].T @ v[:, i * N:(i + 1) * N]
        c = np.minimum(np.maximum(d, -lim[i][:, None]), lim[i][:, None])
        z = xq @ mxq(c, 0, "e4m3")
        y = y + lam[:, i][:, None] * z
    return y

@@ -1,0 +1,272 @@
+from contextlib import ExitStack
+
+import concourse.mybir as mybir
+from concourse.masks import make_identity
+
+M, K, N, R, T = 1024, 1024, 1024, 512, 2
+
+F32 = mybir.dt.float32
+BF16 = mybir.dt.bfloat16
+I32 = mybir.dt.int32
+U32 = mybir.dt.uint32
+U8 = mybir.dt.uint8
+E4M3 = mybir.dt.float8_e4m3fn_x4
+E2M1 = mybir.dt.float4_e2m1fn_x4
+ALU = mybir.AluOpType
+
+FLOPS = 2 * M * K * N * (1 + T) + 2 * T * R * K * N
+
+P = 128
+NH = 512
+MT = M // P
+G = K // 512
+H = N // NH
+VC = 320
+YS = (1, 1, 2, 2, 2, 0, 0, 0)
+
+
+def tile_clipped_task_arithmetic_s4_kernel(
+    tc, x, w_words, w_scales, u_words, u_scales, v_words, v_scales, lim, lam, out
+):
+    nc = tc.nc
+    with ExitStack() as ctx:
+        keep = ctx.enter_context(tc.tile_pool(name="keep", bufs=1))
+        work = ctx.enter_context(tc.tile_pool(name="work", bufs=4))
+        psum_d = ctx.enter_context(tc.psum_pool(name="psum_d", bufs=4))
+        psum_z = ctx.enter_context(tc.psum_pool(name="psum_z", bufs=4))
+        ctx.enter_context(tc.manual_schedule())
+
+        u_raw = [keep.tile([P, 2 * K], U8, name=f"u_raw{i}", align_bytes=64) for i in range(T)]
+        u_ord = [keep.tile([P, G, 4, P, 2], U8, name=f"u_ord{i}", align_bytes=64) for i in range(T)]
+        us_raw = keep.tile([P, T * K], U8, name="us_raw", align_bytes=64)
+        us_ord = [keep.tile([P, G, 4, P], U8, name=f"us_ord{i}", align_bytes=64) for i in range(T)]
+        v_sb = [[keep.tile([P, 2 * NH], U8, name=f"v{i}_{h}", align_bytes=64) for h in range(H)] for i in range(T)]
+        vs_sb = keep.tile([P, T * N], U8, name="vs_sb", align_bytes=64)
+        w_sb = [keep.tile([P, N * 4], U8, name=f"w{g}", align_bytes=64) for g in range(G)]
+        ws_sb = keep.tile([P, G, N], U8, name="ws_sb", align_bytes=64)
+        x_sb = [keep.tile([P, 2, K], BF16, name=f"x{c}", align_bytes=64) for c in range(MT // 2)]
+        xq = [keep.tile([P, 4, P], U32, name=f"xq{c}", align_bytes=64) for c in range(MT // 2)]
+        xs = [keep.tile([P, 4, P], U8, name=f"xs{c}", align_bytes=64) for c in range(MT // 2)]
+        cq = [keep.tile([P, NH], U32, name=f"cq{j}", align_bytes=64) for j in range(8)]
+        cs = [keep.tile([P, NH], U8, name=f"cs{j}", align_bytes=64) for j in range(8)]
+        acc = [[keep.tile([P, NH], F32, name=f"acc{h}_{m}", align_bytes=64) for m in range(MT)] for h in range(H)]
+        ident = keep.tile([P, P], F32, name="ident")
+        lim_bf = keep.tile([P, T, G, 4], BF16, name="lim_bf")
+        lim_hi = keep.tile([P, T * G * 4], F32, name="lim_hi")
+        lim_lo = keep.tile([P, T * G * 4], F32, name="lim_lo")
+        lam_bf = keep.tile([P, MT * T], BF16, name="lam_bf")
+        lam_f = keep.tile([P, MT * T], F32, name="lam_f")
+
+        def load_u(i):
+            nc.sync.dma_start(out=u_raw[i][:].bitcast(I32), in_=u_words[0, :, 2 * K * i : 2 * K * (i + 1)].bitcast(I32))
+
+        def load_v(i, h):
+            c0 = 2 * (N * i + NH * h)
+            nc.sync.dma_start(out=v_sb[i][h][:].bitcast(I32), in_=v_words[0, :, c0 : c0 + 2 * NH].bitcast(I32))
+
+        def load_scales(dst, rows, eng):
+            for q in range(4):
+                eng.dma_start(out=dst[32 * q : 32 * q + 4, :].bitcast(I32), in_=rows[4 * q : 4 * q + 4, :].bitcast(I32))
+
+        nc.vector.memset(us_raw[:].bitcast(I32), 0)
+        nc.vector.memset(vs_sb[:].bitcast(I32), 0)
+        nc.gpsimd.memset(ws_sb[:].rearrange("p g n -> p (g n)").bitcast(I32), 0)
+        load_u(0)
+        load_v(0, 0)
+        load_scales(us_raw, u_scales[0], nc.sync)
+        load_scales(vs_sb, v_scales[0], nc.scalar)
+        nc.gpsimd.dma_start(out=lim_bf[:], in_=lim.rearrange("i (g p t) -> p i g t", g=G, t=4))
+        nc.gpsimd.dma_start(out=lam_bf[:], in_=lam.rearrange("(p m) i -> p (m i)", m=MT))
+        x_view = x.rearrange("(p c m) k -> c p m k", c=MT // 2, m=2)
+        nc.sync.dma_start(out=x_sb[0][:], in_=x_view[0])
+        nc.sync.dma_start(out=x_sb[1][:], in_=x_view[1])
+        load_u(1)
+        load_v(1, 0)
+        nc.sync.dma_start(out=x_sb[2][:], in_=x_view[2])
+        nc.sync.dma_start(out=x_sb[3][:], in_=x_view[3])
+        for q in range(4):
+            nc.sync.dma_start(
+                out=ws_sb[32 * q : 32 * q + 4, :, :].bitcast(I32),
+                in_=w_scales[:, 4 * q : 4 * q + 4, :].rearrange("g r n -> r g n").bitcast(I32),
+            )
+        for g in range(G):
+            nc.sync.dma_start(out=w_sb[g][:].bitcast(I32), in_=w_words[g].rearrange("p n t -> p (n t)").bitcast(I32))
+        load_v(0, 1)
+        load_v(1, 1)
+
+        make_identity(nc, ident[:])
+        nc.gpsimd.tensor_copy(out=lim_hi[:], in_=lim_bf[:].rearrange("p i g t -> p (i g t)"))
+        nc.gpsimd.tensor_scalar(out=lim_lo[:], in0=lim_bf[:].rearrange("p i g t -> p (i g t)"), scalar1=-1.0, scalar2=0.0, op0=ALU.mult, op1=ALU.add)
+        nc.gpsimd.tensor_copy(out=lam_f[:], in_=lam_bf[:])
+
+        units = [(h, i, g) for h in range(H) for i in range(T) for g in range(G)]
+
+        def order_u(i, g, eng):
+            eng.tensor_copy(
+                out=u_ord[i][:, g, :, :, :],
+                in_=u_raw[i][:, 1024 * g : 1024 * (g + 1)].rearrange("p (m t b) -> p t m b", t=4, b=2),
+            )
+            eng.tensor_copy(
+                out=us_ord[i][:, g, :, :],
+                in_=us_raw[:, K * i + 512 * g : K * i + 512 * (g + 1)].rearrange("p (m t) -> p t m", t=4),
+            )
+
+        d_sb = {}
+        grp = {}
+
+        def task_vectors(j, on_vector=(), ts=range(4)):
+            h, i, g = units[j]
+            if j not in d_sb:
+                d_sb[j] = work.tile([P, 4, NH], BF16, name="d_sb", align_bytes=64)
+            for t in ts:
+                ps = psum_d.tile([P, NH], F32, name="ps_d")
+                nc.tensor.matmul_mx(
+                    out=ps[:],
+                    lhsT=u_ord[i][:, g, t, :, :].rearrange("p m b -> p (m b)").bitcast(E2M1),
+                    lhsT_scale=us_ord[i][:, g, t, :],
+                    rhs=v_sb[i][h][:].bitcast(E2M1),
+                    rhs_scale=vs_sb[:, N * i + NH * h : N * i + NH * (h + 1)],
+                    start=True,
+                    stop=True,
+                )
+                if t in on_vector:
+                    clip(j, t, ps[:])
+                else:
+                    nc.scalar.copy(out=d_sb[j][:, t, :], in_=ps[:])
+
+        def clip(j, t, src):
+            h, i, g = units[j]
+            c = (i * G + g) * 4 + t
+            nc.vector.tensor_scalar(
+                out=d_sb[j][:, t, :], in0=src, scalar1=lim_hi[:, c : c + 1], scalar2=lim_lo[:, c : c + 1], op0=ALU.min, op1=ALU.max
+            )
+
+        def clip_rest(j, on_vector):
+            for t in range(4):
+                if t not in on_vector:
+                    clip(j, t, d_sb[j][:, t, :])
+
+        def interleave(j, cols, scalar_cols):
+            grp[j] = work.tile([P, NH, 4], BF16, name="grp", align_bytes=64)
+            if cols > 0:
+                nc.vector.tensor_copy(out=grp[j][:, 0:cols, :], in_=d_sb[j][:, :, 0:cols].rearrange("p t n -> p n t"))
+            if scalar_cols:
+                nc.scalar.copy(out=grp[j][:, cols:NH, :], in_=d_sb[j][:, :, cols:NH].rearrange("p t n -> p n t"))
+
+        def quantize(j):
+            nc.vector.quantize_mx(out=cq[j][:].bitcast(E4M3), scales=cs[j][:], in_=grp[j][:].rearrange("p n t -> p (n t)"))
+
+        xg = {}
+
+        def turn_x(m):
+            c, mm = divmod(m, 2)
+            if mm == 0:
+                xg[c] = work.tile([P, 4, P, 4], BF16, name="xg", align_bytes=64)
+            ps = psum_z.tile([P, G, 2, P], F32, name="ps_z")
+            words = x_sb[c][:, mm, :].bitcast(F32)
+            for g in range(G):
+                for u in range(2):
+                    nc.tensor.transpose(ps[:, g, u, :], words[:, 256 * g + u : 256 * (g + 1) : 2], ident[:])
+            nc.scalar.copy(
+                out=xg[c][:, 2 * mm : 2 * mm + 2, :, :].bitcast(F32),
+                in_=ps[:].rearrange("p g u n -> p g n u"),
+            )
+
+        def quantize_x(c):
+            nc.vector.quantize_mx(
+                out=xq[c][:].rearrange("p a n -> p (a n)").bitcast(E4M3),
+                scales=xs[c][:].rearrange("p a n -> p (a n)"),
+                in_=xg[c][:].rearrange("p a n t -> p (a n t)"),
+            )
+
+        def x_times(m, rhs, rhs_scale):
+            c, mm = divmod(m, 2)
+            ps = psum_z.tile([P, NH], F32, name="ps_z")
+            for g in range(G):
+                nc.tensor.matmul_mx(
+                    out=ps[:],
+                    lhsT=xq[c][:, 2 * mm + g, :].bitcast(E4M3),
+                    lhsT_scale=xs[c][:, 2 * mm + g, :],
+                    rhs=rhs[g],
+                    rhs_scale=rhs_scale[g],
+                    start=(g == 0),
+                    stop=(g == G - 1),
+                )
+            return ps
+
+        def base(h, m):
+            ps = x_times(
+                m,
+                [w_sb[g][:, 4 * NH * h : 4 * NH * (h + 1)].bitcast(E4M3) for g in range(G)],
+                [ws_sb[:, g, NH * h : NH * (h + 1)] for g in range(G)],
+            )
+            nc.scalar.copy(out=acc[h][m][:], in_=ps[:])
+
+        out_view = out.rearrange("(p m) n -> m p n", m=MT)
+
+        def task(pair, m):
+            h, i = divmod(pair, T)
+            ps = x_times(
+                m,
+                [cq[2 * pair + g][:].bitcast(E4M3) for g in range(G)],
+                [cs[2 * pair + g][:] for g in range(G)],
+            )
+            nc.vector.scalar_tensor_tensor(
+                out=acc[h][m][:], in0=ps[:], scalar=lam_f[:, m * T + i : m * T + i + 1], in1=acc[h][m][:], op0=ALU.mult, op1=ALU.add
+            )
+            if i == T - 1:
+                nc.sync.dma_start(out=out_view[m][:, NH * h : NH * (h + 1)], in_=acc[h][m][:])
+
+        order_u(0, 0, nc.vector)
+        order_u(0, 1, nc.vector)
+        order_u(1, 0, nc.gpsimd)
+        order_u(1, 1, nc.gpsimd)
+        both = (1, 3)
+        task_vectors(0, both)
+        task_vectors(1, both)
+        for m in range(0, 4):
+            turn_x(m)
+        clip_rest(0, both)
+        clip_rest(1, both)
+        quantize_x(0)
+        interleave(0, 512, False)
+        quantize_x(1)
+        quantize(0)
+        for m in range(4, 8):
+            turn_x(m)
+        interleave(1, 512, False)
+        quantize_x(2)
+        quantize(1)
+        quantize_x(3)
+        task_vectors(2, both)
+        clip_rest(2, both)
+        base(0, 0)
+        interleave(2, 512, False)
+        base(0, 1)
+        task_vectors(3, both)
+        base(0, 2)
+        quantize(2)
+        for m in range(3, 8):
+            base(0, m)
+        ym = 0
+        for k in range(8):
+            pair, first = divmod(k, 2)
+            ms = range(4 * first, 4 * first + 4)
+            j = k + 3
+            if j < 8:
+                clip_rest(j, both if j == 3 else ())
+            task(pair, ms[0])
+            if j + 1 < 8:
+                task_vectors(j + 1, (), (0, 1))
+            if j < 8:
+                interleave(j, VC, VC < NH)
+            task(pair, ms[1])
+            if j + 1 < 8:
+                task_vectors(j + 1, (), (2, 3))
+            task(pair, ms[2])
+            if j < 8:
+                quantize(j)
+            for r in range(YS[k]):
+                base(1, ym)
+                ym += 1
+            task(pair, ms[3])

@@ -21,7 +21,9 @@ NH = 512
 MT = M // P
 G = K // 512
 H = N // NH
-VC = 320
+VC = 288
+VI = 512
+WARM = 32
 YS = (1, 1, 2, 2, 2, 0, 0, 0)
 
 
@@ -50,6 +52,9 @@ def tile_clipped_task_arithmetic_s4_kernel(
         cq = [keep.tile([P, NH], U32, name=f"cq{j}", align_bytes=64) for j in range(8)]
         cs = [keep.tile([P, NH], U8, name=f"cs{j}", align_bytes=64) for j in range(8)]
         acc = [[keep.tile([P, NH], F32, name=f"acc{h}_{m}", align_bytes=64) for m in range(MT)] for h in range(H)]
+        warm = keep.tile([P, 4 * P], BF16, name="warm", align_bytes=64)
+        warm_q = keep.tile([P, P], U32, name="warm_q", align_bytes=64)
+        warm_s = keep.tile([P, P], U8, name="warm_s", align_bytes=64)
         ident = keep.tile([P, P], F32, name="ident")
         lim_bf = keep.tile([P, T, G, 4], BF16, name="lim_bf")
         lim_hi = keep.tile([P, T * G * 4], F32, name="lim_hi")
@@ -57,31 +62,33 @@ def tile_clipped_task_arithmetic_s4_kernel(
         lam_bf = keep.tile([P, MT * T], BF16, name="lam_bf")
         lam_f = keep.tile([P, MT * T], F32, name="lam_f")
 
-        def load_u(i):
-            nc.sync.dma_start(out=u_raw[i][:].bitcast(I32), in_=u_words[0, :, 2 * K * i : 2 * K * (i + 1)].bitcast(I32))
+        def load_u(i, eng):
+            eng.dma_start(out=u_raw[i][:].bitcast(I32), in_=u_words[0, :, 2 * K * i : 2 * K * (i + 1)].bitcast(I32))
 
-        def load_v(i, h):
+        def load_v(i, h, eng):
             c0 = 2 * (N * i + NH * h)
-            nc.sync.dma_start(out=v_sb[i][h][:].bitcast(I32), in_=v_words[0, :, c0 : c0 + 2 * NH].bitcast(I32))
+            eng.dma_start(out=v_sb[i][h][:].bitcast(I32), in_=v_words[0, :, c0 : c0 + 2 * NH].bitcast(I32))
 
-        def load_scales(dst, rows, eng):
+        def load_scales(dst, rows, engines):
             for q in range(4):
-                eng.dma_start(out=dst[32 * q : 32 * q + 4, :].bitcast(I32), in_=rows[4 * q : 4 * q + 4, :].bitcast(I32))
+                engines[q].dma_start(out=dst[32 * q : 32 * q + 4, :].bitcast(I32), in_=rows[4 * q : 4 * q + 4, :].bitcast(I32))
 
         nc.vector.memset(us_raw[:].bitcast(I32), 0)
         nc.vector.memset(vs_sb[:].bitcast(I32), 0)
-        nc.gpsimd.memset(ws_sb[:].rearrange("p g n -> p (g n)").bitcast(I32), 0)
-        load_u(0)
-        load_v(0, 0)
-        load_scales(us_raw, u_scales[0], nc.sync)
-        load_scales(vs_sb, v_scales[0], nc.scalar)
+        load_u(0, nc.sync)
+        load_v(0, 0, nc.scalar)
+        load_scales(us_raw, u_scales[0], [nc.sync] * 4)
+        load_scales(vs_sb, v_scales[0], [nc.scalar, nc.scalar, nc.gpsimd, nc.gpsimd])
+        nc.vector.memset(warm[:].bitcast(I32), 0)
         nc.gpsimd.dma_start(out=lim_bf[:], in_=lim.rearrange("i (g p t) -> p i g t", g=G, t=4))
+        load_u(1, nc.gpsimd)
+        make_identity(nc, ident[:])
+        nc.gpsimd.memset(ws_sb[:].rearrange("p g n -> p (g n)").bitcast(I32), 0)
         nc.gpsimd.dma_start(out=lam_bf[:], in_=lam.rearrange("(p m) i -> p (m i)", m=MT))
         x_view = x.rearrange("(p c m) k -> c p m k", c=MT // 2, m=2)
         nc.sync.dma_start(out=x_sb[0][:], in_=x_view[0])
         nc.sync.dma_start(out=x_sb[1][:], in_=x_view[1])
-        load_u(1)
-        load_v(1, 0)
+        load_v(1, 0, nc.sync)
         nc.sync.dma_start(out=x_sb[2][:], in_=x_view[2])
         nc.sync.dma_start(out=x_sb[3][:], in_=x_view[3])
         for q in range(4):
@@ -91,10 +98,9 @@ def tile_clipped_task_arithmetic_s4_kernel(
             )
         for g in range(G):
             nc.sync.dma_start(out=w_sb[g][:].bitcast(I32), in_=w_words[g].rearrange("p n t -> p (n t)").bitcast(I32))
-        load_v(0, 1)
-        load_v(1, 1)
+        load_v(0, 1, nc.sync)
+        load_v(1, 1, nc.sync)
 
-        make_identity(nc, ident[:])
         nc.gpsimd.tensor_copy(out=lim_hi[:], in_=lim_bf[:].rearrange("p i g t -> p (i g t)"))
         nc.gpsimd.tensor_scalar(out=lim_lo[:], in0=lim_bf[:].rearrange("p i g t -> p (i g t)"), scalar1=-1.0, scalar2=0.0, op0=ALU.mult, op1=ALU.add)
         nc.gpsimd.tensor_copy(out=lam_f[:], in_=lam_bf[:])
@@ -149,9 +155,13 @@ def tile_clipped_task_arithmetic_s4_kernel(
         def interleave(j, cols, scalar_cols):
             grp[j] = work.tile([P, NH, 4], BF16, name="grp", align_bytes=64)
             if cols > 0:
-                nc.vector.tensor_copy(out=grp[j][:, 0:cols, :], in_=d_sb[j][:, :, 0:cols].rearrange("p t n -> p n t"))
+                nc.vector.tensor_copy(
+                    out=grp[j][:, 0:cols, :].rearrange("p (c i) t -> p c t i", i=4), in_=d_sb[j][:, :, 0:cols].rearrange("p t (c i) -> p c t i", i=4)
+                )
             if scalar_cols:
-                nc.scalar.copy(out=grp[j][:, cols:NH, :], in_=d_sb[j][:, :, cols:NH].rearrange("p t n -> p n t"))
+                nc.scalar.copy(
+                    out=grp[j][:, cols:NH, :].rearrange("p (c i) t -> p c t i", i=4), in_=d_sb[j][:, :, cols:NH].rearrange("p t (c i) -> p c t i", i=4)
+                )
 
         def quantize(j):
             nc.vector.quantize_mx(out=cq[j][:].bitcast(E4M3), scales=cs[j][:], in_=grp[j][:].rearrange("p n t -> p (n t)"))
@@ -211,16 +221,19 @@ def tile_clipped_task_arithmetic_s4_kernel(
                 [cq[2 * pair + g][:].bitcast(E4M3) for g in range(G)],
                 [cs[2 * pair + g][:] for g in range(G)],
             )
-            nc.vector.scalar_tensor_tensor(
-                out=acc[h][m][:], in0=ps[:], scalar=lam_f[:, m * T + i : m * T + i + 1], in1=acc[h][m][:], op0=ALU.mult, op1=ALU.add
-            )
+            lam_col = lam_f[:, m * T + i : m * T + i + 1]
+            nc.vector.scalar_tensor_tensor(out=acc[h][m][:], in0=ps[:], scalar=lam_col, in1=acc[h][m][:], op0=ALU.mult, op1=ALU.add)
             if i == T - 1:
                 nc.sync.dma_start(out=out_view[m][:, NH * h : NH * (h + 1)], in_=acc[h][m][:])
 
+        nc.vector.quantize_mx(out=warm_q[:].bitcast(E4M3), scales=warm_s[:], in_=warm[:])
+        ps_warm = psum_z.tile([P, NH], F32, name="ps_z")
+        for r in range(WARM):
+            nc.tensor.matmul_mx(
+                out=ps_warm[:, 0:P], lhsT=warm_q[:].bitcast(E4M3), lhsT_scale=warm_s[:], rhs=warm_q[:].bitcast(E4M3), rhs_scale=warm_s[:], start=True, stop=True
+            )
         order_u(0, 0, nc.vector)
         order_u(0, 1, nc.vector)
-        order_u(1, 0, nc.gpsimd)
-        order_u(1, 1, nc.gpsimd)
         both = (1, 3)
         task_vectors(0, both)
         task_vectors(1, both)
@@ -228,6 +241,8 @@ def tile_clipped_task_arithmetic_s4_kernel(
             turn_x(m)
         clip_rest(0, both)
         clip_rest(1, both)
+        order_u(1, 0, nc.vector)
+        order_u(1, 1, nc.vector)
         quantize_x(0)
         interleave(0, 512, False)
         quantize_x(1)
@@ -238,15 +253,14 @@ def tile_clipped_task_arithmetic_s4_kernel(
         quantize_x(2)
         quantize(1)
         quantize_x(3)
-        task_vectors(2, both)
-        clip_rest(2, both)
+        task_vectors(2)
+        clip_rest(2, ())
         base(0, 0)
-        interleave(2, 512, False)
-        base(0, 1)
-        task_vectors(3, both)
-        base(0, 2)
-        quantize(2)
-        for m in range(3, 8):
+        interleave(2, VI, VI < NH)
+        for m in range(1, 8):
+            if m == 2:
+                task_vectors(3, both)
+                quantize(2)
             base(0, m)
         ym = 0
         for k in range(8):

@@ -13,6 +13,7 @@ U8 = mybir.dt.uint8
 E4M3 = mybir.dt.float8_e4m3fn_x4
 E2M1 = mybir.dt.float4_e2m1fn_x4
 ALU = mybir.AluOpType
+ACT = mybir.ActivationFunctionType
 
 FLOPS = 2 * M * K * N * (1 + T) + 2 * T * R * K * N
 
@@ -21,10 +22,12 @@ NH = 512
 MT = M // P
 G = K // 512
 H = N // NH
-VC = 288
-VI = 512
+VCS = (512, 512, 512, 256, 256, 256, 256, 256)
+ONV = ((), (0, 2), (), (0, 2), (), (), (), ())
+POS = 4
 WARM = 32
-YS = (1, 1, 2, 2, 2, 0, 0, 0)
+SG = ((4, 0), (4, 3), (5, 0), (5, 2), (6, 3))
+YS = (2, 2, 2, 2, 0, 0, 0, 0)
 
 
 def tile_clipped_task_arithmetic_s4_kernel(
@@ -55,6 +58,7 @@ def tile_clipped_task_arithmetic_s4_kernel(
         warm = keep.tile([P, 4 * P], BF16, name="warm", align_bytes=64)
         warm_q = keep.tile([P, P], U32, name="warm_q", align_bytes=64)
         warm_s = keep.tile([P, P], U8, name="warm_s", align_bytes=64)
+        act_dummy = keep.tile([P, 1], F32, name="act_dummy")
         ident = keep.tile([P, P], F32, name="ident")
         lim_bf = keep.tile([P, T, G, 4], BF16, name="lim_bf")
         lim_hi = keep.tile([P, T * G * 4], F32, name="lim_hi")
@@ -75,16 +79,15 @@ def tile_clipped_task_arithmetic_s4_kernel(
 
         nc.vector.memset(us_raw[:].bitcast(I32), 0)
         nc.vector.memset(vs_sb[:].bitcast(I32), 0)
-        load_u(0, nc.sync)
-        load_v(0, 0, nc.scalar)
+        load_u(0, nc.gpsimd)
+        load_v(0, 0, nc.gpsimd)
         load_scales(us_raw, u_scales[0], [nc.sync] * 4)
-        load_scales(vs_sb, v_scales[0], [nc.scalar, nc.scalar, nc.gpsimd, nc.gpsimd])
+        load_scales(vs_sb, v_scales[0], [nc.scalar] * 4)
+        nc.scalar.dma_start(out=lim_bf[:], in_=lim.rearrange("i (g p t) -> p i g t", g=G, t=4))
         nc.vector.memset(warm[:].bitcast(I32), 0)
-        nc.gpsimd.dma_start(out=lim_bf[:], in_=lim.rearrange("i (g p t) -> p i g t", g=G, t=4))
-        load_u(1, nc.gpsimd)
         make_identity(nc, ident[:])
+        load_u(1, nc.gpsimd)
         nc.gpsimd.memset(ws_sb[:].rearrange("p g n -> p (g n)").bitcast(I32), 0)
-        nc.gpsimd.dma_start(out=lam_bf[:], in_=lam.rearrange("(p m) i -> p (m i)", m=MT))
         x_view = x.rearrange("(p c m) k -> c p m k", c=MT // 2, m=2)
         nc.sync.dma_start(out=x_sb[0][:], in_=x_view[0])
         nc.sync.dma_start(out=x_sb[1][:], in_=x_view[1])
@@ -98,11 +101,10 @@ def tile_clipped_task_arithmetic_s4_kernel(
             )
         for g in range(G):
             nc.sync.dma_start(out=w_sb[g][:].bitcast(I32), in_=w_words[g].rearrange("p n t -> p (n t)").bitcast(I32))
+        nc.sync.dma_start(out=lam_bf[:], in_=lam.rearrange("(p m) i -> p (m i)", m=MT))
         load_v(0, 1, nc.sync)
         load_v(1, 1, nc.sync)
 
-        nc.gpsimd.tensor_copy(out=lim_hi[:], in_=lim_bf[:].rearrange("p i g t -> p (i g t)"))
-        nc.gpsimd.tensor_scalar(out=lim_lo[:], in0=lim_bf[:].rearrange("p i g t -> p (i g t)"), scalar1=-1.0, scalar2=0.0, op0=ALU.mult, op1=ALU.add)
         nc.gpsimd.tensor_copy(out=lam_f[:], in_=lam_bf[:])
 
         units = [(h, i, g) for h in range(H) for i in range(T) for g in range(G)]
@@ -189,16 +191,16 @@ def tile_clipped_task_arithmetic_s4_kernel(
                 in_=xg[c][:].rearrange("p a n t -> p (a n t)"),
             )
 
-        def x_times(m, rhs, rhs_scale):
+        def x_times(m, rhs, rhs_scale, cols=slice(0, NH)):
             c, mm = divmod(m, 2)
             ps = psum_z.tile([P, NH], F32, name="ps_z")
             for g in range(G):
                 nc.tensor.matmul_mx(
-                    out=ps[:],
+                    out=ps[:, cols],
                     lhsT=xq[c][:, 2 * mm + g, :].bitcast(E4M3),
                     lhsT_scale=xs[c][:, 2 * mm + g, :],
-                    rhs=rhs[g],
-                    rhs_scale=rhs_scale[g],
+                    rhs=rhs[g][:, cols].bitcast(E4M3),
+                    rhs_scale=rhs_scale[g][:, cols],
                     start=(g == 0),
                     stop=(g == G - 1),
                 )
@@ -207,25 +209,42 @@ def tile_clipped_task_arithmetic_s4_kernel(
         def base(h, m):
             ps = x_times(
                 m,
-                [w_sb[g][:, 4 * NH * h : 4 * NH * (h + 1)].bitcast(E4M3) for g in range(G)],
+                [w_sb[g][:].bitcast(U32)[:, NH * h : NH * (h + 1)] for g in range(G)],
                 [ws_sb[:, g, NH * h : NH * (h + 1)] for g in range(G)],
             )
             nc.scalar.copy(out=acc[h][m][:], in_=ps[:])
 
         out_view = out.rearrange("(p m) n -> m p n", m=MT)
 
-        def task(pair, m):
+        late = []
+
+        def task(pair, m, on_scalar=False, cols=slice(0, NH)):
             h, i = divmod(pair, T)
             ps = x_times(
                 m,
-                [cq[2 * pair + g][:].bitcast(E4M3) for g in range(G)],
-                [cs[2 * pair + g][:] for g in range(G)],
+                [cq[2 * pair + g] for g in range(G)],
+                [cs[2 * pair + g] for g in range(G)],
+                cols,
             )
             lam_col = lam_f[:, m * T + i : m * T + i + 1]
-            nc.vector.scalar_tensor_tensor(out=acc[h][m][:], in0=ps[:], scalar=lam_col, in1=acc[h][m][:], op0=ALU.mult, op1=ALU.add)
+            if on_scalar:
+                part = work.tile([P, NH], F32, name="part", align_bytes=64)
+                nc.scalar.activation(out=part[:], in_=ps[:], func=ACT.Copy, scale=lam_col)
+                nc.gpsimd.tensor_tensor(out=acc[h][m][:], in0=acc[h][m][:], in1=part[:], op=ALU.add)
+            else:
+                nc.vector.scalar_tensor_tensor(out=acc[h][m][:, cols], in0=ps[:, cols], scalar=lam_col, in1=acc[h][m][:, cols], op0=ALU.mult, op1=ALU.add)
             if i == T - 1:
-                nc.sync.dma_start(out=out_view[m][:, NH * h : NH * (h + 1)], in_=acc[h][m][:])
+                late.append((h, m, cols))
+                if not on_scalar:
+                    store(late.pop())
+                    if len(late) > 0 and m - late[0][1] >= 2:
+                        store(late.pop(0))
 
+        def store(hm):
+            h, m, cols = hm
+            nc.sync.dma_start(out=out_view[m][:, NH * h + cols.start : NH * h + cols.stop], in_=acc[h][m][:, cols])
+
+        nc.scalar.activation(out=act_dummy[:], in_=warm[:, 0:1], func=ACT.Copy, scale=1.0)
         nc.vector.quantize_mx(out=warm_q[:].bitcast(E4M3), scales=warm_s[:], in_=warm[:])
         ps_warm = psum_z.tile([P, NH], F32, name="ps_z")
         for r in range(WARM):
@@ -234,32 +253,34 @@ def tile_clipped_task_arithmetic_s4_kernel(
             )
         order_u(0, 0, nc.vector)
         order_u(0, 1, nc.vector)
-        both = (1, 3)
-        task_vectors(0, both)
-        task_vectors(1, both)
+        lim_cols = lim_bf[:].rearrange("p i g t -> p (i g t)")
+        nc.vector.tensor_copy(out=lim_hi[:], in_=lim_cols)
+        nc.vector.tensor_scalar(out=lim_lo[:], in0=lim_cols, scalar1=-1.0, scalar2=None, op0=ALU.mult)
+        task_vectors(0, ONV[0])
+        task_vectors(1, ONV[1])
         for m in range(0, 4):
             turn_x(m)
-        clip_rest(0, both)
-        clip_rest(1, both)
+        clip_rest(0, ONV[0])
+        clip_rest(1, ONV[1])
         order_u(1, 0, nc.vector)
         order_u(1, 1, nc.vector)
         quantize_x(0)
-        interleave(0, 512, False)
+        interleave(0, VCS[0], VCS[0] < NH)
         quantize_x(1)
         quantize(0)
         for m in range(4, 8):
             turn_x(m)
-        interleave(1, 512, False)
+        interleave(1, VCS[1], VCS[1] < NH)
         quantize_x(2)
         quantize(1)
         quantize_x(3)
-        task_vectors(2)
-        clip_rest(2, ())
+        task_vectors(2, ONV[2])
+        clip_rest(2, ONV[2])
         base(0, 0)
-        interleave(2, VI, VI < NH)
+        interleave(2, VCS[2], VCS[2] < NH)
         for m in range(1, 8):
-            if m == 2:
-                task_vectors(3, both)
+            if m == POS:
+                task_vectors(3, ONV[3])
                 quantize(2)
             base(0, m)
         ym = 0
@@ -268,19 +289,25 @@ def tile_clipped_task_arithmetic_s4_kernel(
             ms = range(4 * first, 4 * first + 4)
             j = k + 3
             if j < 8:
-                clip_rest(j, both if j == 3 else ())
-            task(pair, ms[0])
+                clip_rest(j, ONV[j])
+            task(pair, ms[0], (k, 0) in SG)
             if j + 1 < 8:
-                task_vectors(j + 1, (), (0, 1))
+                task_vectors(j + 1, ONV[j + 1], (0, 1))
             if j < 8:
-                interleave(j, VC, VC < NH)
-            task(pair, ms[1])
+                interleave(j, VCS[j], VCS[j] < NH)
+            task(pair, ms[1], (k, 1) in SG)
             if j + 1 < 8:
-                task_vectors(j + 1, (), (2, 3))
-            task(pair, ms[2])
+                task_vectors(j + 1, ONV[j + 1], (2, 3))
+            task(pair, ms[2], (k, 2) in SG)
             if j < 8:
                 quantize(j)
             for r in range(YS[k]):
                 base(1, ym)
                 ym += 1
-            task(pair, ms[3])
+            if k < 7:
+                task(pair, ms[3], (k, 3) in SG)
+            else:
+                task(pair, ms[3], cols=slice(0, NH // 2))
+                task(pair, ms[3], cols=slice(NH // 2, NH))
+        for hm in late:
+            store(hm)

@@ -23,9 +23,9 @@ MT = M // P
 G = K // 512
 H = N // NH
 VCS = (512, 512, 512, 256, 256, 256, 256, 256)
-ONV = ((), (0, 2), (), (0, 2), (), (), (), ())
+ONV = ((3,), (1, 3), (), (1, 3), (), (), (), ())
 POS = 4
-WARM = 32
+WARM = (24, 8)
 SG = ((4, 0), (4, 3), (5, 0), (5, 2), (6, 3))
 YS = (2, 2, 2, 2, 0, 0, 0, 0)
 
@@ -79,28 +79,38 @@ def tile_clipped_task_arithmetic_s4_kernel(
 
         nc.vector.memset(us_raw[:].bitcast(I32), 0)
         nc.vector.memset(vs_sb[:].bitcast(I32), 0)
+        nc.vector.memset(warm[:].bitcast(I32), 0)
+        nc.vector.quantize_mx(out=warm_q[:].bitcast(E4M3), scales=warm_s[:], in_=warm[:])
+        nc.vector.memset(ws_sb[:].rearrange("p g n -> p (g n)").bitcast(I32), 0)
+        x_view = x.rearrange("(p c m) k -> c p m k", c=MT // 2, m=2)
+
+        def load_x(c):
+            nc.sync.dma_start(out=x_sb[c][:], in_=x_view[c])
+
+        def load_w(g):
+            nc.sync.dma_start(out=w_sb[g][:].bitcast(I32), in_=w_words[g].rearrange("p n t -> p (n t)").bitcast(I32))
+
+        nc.gpsimd.dma_start(out=x_sb[0][:], in_=x_view[0])
         load_u(0, nc.gpsimd)
         load_v(0, 0, nc.gpsimd)
-        load_scales(us_raw, u_scales[0], [nc.sync] * 4)
-        load_scales(vs_sb, v_scales[0], [nc.scalar] * 4)
-        nc.scalar.dma_start(out=lim_bf[:], in_=lim.rearrange("i (g p t) -> p i g t", g=G, t=4))
-        nc.vector.memset(warm[:].bitcast(I32), 0)
         make_identity(nc, ident[:])
-        load_u(1, nc.gpsimd)
-        nc.gpsimd.memset(ws_sb[:].rearrange("p g n -> p (g n)").bitcast(I32), 0)
-        x_view = x.rearrange("(p c m) k -> c p m k", c=MT // 2, m=2)
-        nc.sync.dma_start(out=x_sb[0][:], in_=x_view[0])
-        nc.sync.dma_start(out=x_sb[1][:], in_=x_view[1])
+        nc.gpsimd.dma_start(out=x_sb[1][:], in_=x_view[1])
+        for q in range(4):
+            nc.sync.dma_start(out=us_raw[32 * q : 32 * q + 4, :].bitcast(I32), in_=u_scales[0, 4 * q : 4 * q + 4, :].bitcast(I32))
+        for q in range(4):
+            nc.scalar.dma_start(out=vs_sb[32 * q : 32 * q + 4, :].bitcast(I32), in_=v_scales[0, 4 * q : 4 * q + 4, :].bitcast(I32))
+        nc.sync.dma_start(out=lim_bf[:], in_=lim.rearrange("i (g p t) -> p i g t", g=G, t=4))
+        load_x(2)
+        load_u(1, nc.sync)
         load_v(1, 0, nc.sync)
-        nc.sync.dma_start(out=x_sb[2][:], in_=x_view[2])
-        nc.sync.dma_start(out=x_sb[3][:], in_=x_view[3])
+        load_x(3)
         for q in range(4):
             nc.sync.dma_start(
                 out=ws_sb[32 * q : 32 * q + 4, :, :].bitcast(I32),
                 in_=w_scales[:, 4 * q : 4 * q + 4, :].rearrange("g r n -> r g n").bitcast(I32),
             )
-        for g in range(G):
-            nc.sync.dma_start(out=w_sb[g][:].bitcast(I32), in_=w_words[g].rearrange("p n t -> p (n t)").bitcast(I32))
+        load_w(0)
+        load_w(1)
         nc.sync.dma_start(out=lam_bf[:], in_=lam.rearrange("(p m) i -> p (m i)", m=MT))
         load_v(0, 1, nc.sync)
         load_v(1, 1, nc.sync)
@@ -157,13 +167,9 @@ def tile_clipped_task_arithmetic_s4_kernel(
         def interleave(j, cols, scalar_cols):
             grp[j] = work.tile([P, NH, 4], BF16, name="grp", align_bytes=64)
             if cols > 0:
-                nc.vector.tensor_copy(
-                    out=grp[j][:, 0:cols, :].rearrange("p (c i) t -> p c t i", i=4), in_=d_sb[j][:, :, 0:cols].rearrange("p t (c i) -> p c t i", i=4)
-                )
+                nc.vector.tensor_copy(out=grp[j][:, 0:cols, :], in_=d_sb[j][:, :, 0:cols].rearrange("p t n -> p n t"))
             if scalar_cols:
-                nc.scalar.copy(
-                    out=grp[j][:, cols:NH, :].rearrange("p (c i) t -> p c t i", i=4), in_=d_sb[j][:, :, cols:NH].rearrange("p t (c i) -> p c t i", i=4)
-                )
+                nc.scalar.copy(out=grp[j][:, cols:NH, :], in_=d_sb[j][:, :, cols:NH].rearrange("p t n -> p n t"))
 
         def quantize(j):
             nc.vector.quantize_mx(out=cq[j][:].bitcast(E4M3), scales=cs[j][:], in_=grp[j][:].rearrange("p n t -> p (n t)"))
@@ -245,32 +251,38 @@ def tile_clipped_task_arithmetic_s4_kernel(
             nc.sync.dma_start(out=out_view[m][:, NH * h + cols.start : NH * h + cols.stop], in_=acc[h][m][:, cols])
 
         nc.scalar.activation(out=act_dummy[:], in_=warm[:, 0:1], func=ACT.Copy, scale=1.0)
-        nc.vector.quantize_mx(out=warm_q[:].bitcast(E4M3), scales=warm_s[:], in_=warm[:])
-        ps_warm = psum_z.tile([P, NH], F32, name="ps_z")
-        for r in range(WARM):
-            nc.tensor.matmul_mx(
-                out=ps_warm[:, 0:P], lhsT=warm_q[:].bitcast(E4M3), lhsT_scale=warm_s[:], rhs=warm_q[:].bitcast(E4M3), rhs_scale=warm_s[:], start=True, stop=True
-            )
+        ps_warm = psum_d.tile([P, NH], F32, name="ps_d")
+
+        def keep_warm(passes):
+            for r in range(passes):
+                nc.tensor.matmul_mx(
+                    out=ps_warm[:, 0:P], lhsT=warm_q[:].bitcast(E4M3), lhsT_scale=warm_s[:], rhs=warm_q[:].bitcast(E4M3), rhs_scale=warm_s[:], start=True, stop=True
+                )
+
+        keep_warm(WARM[0])
         order_u(0, 0, nc.vector)
         order_u(0, 1, nc.vector)
+        turn_x(0)
+        turn_x(1)
+        keep_warm(WARM[1])
+        quantize_x(0)
         lim_cols = lim_bf[:].rearrange("p i g t -> p (i g t)")
         nc.vector.tensor_copy(out=lim_hi[:], in_=lim_cols)
         nc.vector.tensor_scalar(out=lim_lo[:], in0=lim_cols, scalar1=-1.0, scalar2=None, op0=ALU.mult)
         task_vectors(0, ONV[0])
+        turn_x(2)
+        turn_x(3)
         task_vectors(1, ONV[1])
-        for m in range(0, 4):
-            turn_x(m)
         clip_rest(0, ONV[0])
-        clip_rest(1, ONV[1])
         order_u(1, 0, nc.vector)
-        order_u(1, 1, nc.vector)
-        quantize_x(0)
         interleave(0, VCS[0], VCS[0] < NH)
         quantize_x(1)
+        clip_rest(1, ONV[1])
         quantize(0)
         for m in range(4, 8):
             turn_x(m)
         interleave(1, VCS[1], VCS[1] < NH)
+        order_u(1, 1, nc.vector)
         quantize_x(2)
         quantize(1)
         quantize_x(3)

@@ -22,12 +22,13 @@ NH = 512
 MT = M // P
 G = K // 512
 H = N // NH
-VCS = (512, 512, 512, 256, 256, 256, 256, 256)
-ONV = ((3,), (1, 3), (), (1, 3), (), (), (), ())
+VCS = (512, 512, 512, 256, 224, 224, 192, 128)
+ONV = ((), (1, 2), (), (1, 2), (), (), (), ())
 POS = 4
-WARM = (24, 8)
-SG = ((4, 0), (4, 3), (5, 0), (5, 2), (6, 3))
-YS = (2, 2, 2, 2, 0, 0, 0, 0)
+GCL = ()
+WARM = 24
+SG = ()
+YS = (1, 2, 1, 2, 2, 0, 0, 0)
 
 
 def tile_clipped_task_arithmetic_s4_kernel(
@@ -80,8 +81,6 @@ def tile_clipped_task_arithmetic_s4_kernel(
         nc.vector.memset(us_raw[:].bitcast(I32), 0)
         nc.vector.memset(vs_sb[:].bitcast(I32), 0)
         nc.vector.memset(warm[:].bitcast(I32), 0)
-        nc.vector.quantize_mx(out=warm_q[:].bitcast(E4M3), scales=warm_s[:], in_=warm[:])
-        nc.vector.memset(ws_sb[:].rearrange("p g n -> p (g n)").bitcast(I32), 0)
         x_view = x.rearrange("(p c m) k -> c p m k", c=MT // 2, m=2)
 
         def load_x(c):
@@ -90,19 +89,20 @@ def tile_clipped_task_arithmetic_s4_kernel(
         def load_w(g):
             nc.sync.dma_start(out=w_sb[g][:].bitcast(I32), in_=w_words[g].rearrange("p n t -> p (n t)").bitcast(I32))
 
-        nc.gpsimd.dma_start(out=x_sb[0][:], in_=x_view[0])
-        load_u(0, nc.gpsimd)
-        load_v(0, 0, nc.gpsimd)
+        nc.gpsimd.memset(ws_sb[:].rearrange("p g n -> p (g n)").bitcast(I32), 0)
+        nc.gpsimd.dma_start(out=lim_bf[:], in_=lim.rearrange("i (g p t) -> p i g t", g=G, t=4))
         make_identity(nc, ident[:])
-        nc.gpsimd.dma_start(out=x_sb[1][:], in_=x_view[1])
+        load_u(0, nc.sync)
+        load_v(0, 0, nc.sync)
         for q in range(4):
             nc.sync.dma_start(out=us_raw[32 * q : 32 * q + 4, :].bitcast(I32), in_=u_scales[0, 4 * q : 4 * q + 4, :].bitcast(I32))
         for q in range(4):
             nc.scalar.dma_start(out=vs_sb[32 * q : 32 * q + 4, :].bitcast(I32), in_=v_scales[0, 4 * q : 4 * q + 4, :].bitcast(I32))
-        nc.sync.dma_start(out=lim_bf[:], in_=lim.rearrange("i (g p t) -> p i g t", g=G, t=4))
-        load_x(2)
+        load_x(0)
+        load_x(1)
         load_u(1, nc.sync)
         load_v(1, 0, nc.sync)
+        load_x(2)
         load_x(3)
         for q in range(4):
             nc.sync.dma_start(
@@ -155,7 +155,8 @@ def tile_clipped_task_arithmetic_s4_kernel(
         def clip(j, t, src):
             h, i, g = units[j]
             c = (i * G + g) * 4 + t
-            nc.vector.tensor_scalar(
+            eng = nc.gpsimd if (j, t) in GCL else nc.vector
+            eng.tensor_scalar(
                 out=d_sb[j][:, t, :], in0=src, scalar1=lim_hi[:, c : c + 1], scalar2=lim_lo[:, c : c + 1], op0=ALU.min, op1=ALU.max
             )
 
@@ -167,9 +168,13 @@ def tile_clipped_task_arithmetic_s4_kernel(
         def interleave(j, cols, scalar_cols):
             grp[j] = work.tile([P, NH, 4], BF16, name="grp", align_bytes=64)
             if cols > 0:
-                nc.vector.tensor_copy(out=grp[j][:, 0:cols, :], in_=d_sb[j][:, :, 0:cols].rearrange("p t n -> p n t"))
+                nc.vector.tensor_copy(
+                    out=grp[j][:, 0:cols, :].rearrange("p (c i) t -> p c t i", i=4), in_=d_sb[j][:, :, 0:cols].rearrange("p t (c i) -> p c t i", i=4)
+                )
             if scalar_cols:
-                nc.scalar.copy(out=grp[j][:, cols:NH, :], in_=d_sb[j][:, :, cols:NH].rearrange("p t n -> p n t"))
+                nc.scalar.copy(
+                    out=grp[j][:, cols:NH, :].rearrange("p (c i) t -> p c t i", i=4), in_=d_sb[j][:, :, cols:NH].rearrange("p t (c i) -> p c t i", i=4)
+                )
 
         def quantize(j):
             nc.vector.quantize_mx(out=cq[j][:].bitcast(E4M3), scales=cs[j][:], in_=grp[j][:].rearrange("p n t -> p (n t)"))
@@ -251,6 +256,7 @@ def tile_clipped_task_arithmetic_s4_kernel(
             nc.sync.dma_start(out=out_view[m][:, NH * h + cols.start : NH * h + cols.stop], in_=acc[h][m][:, cols])
 
         nc.scalar.activation(out=act_dummy[:], in_=warm[:, 0:1], func=ACT.Copy, scale=1.0)
+        nc.vector.quantize_mx(out=warm_q[:].bitcast(E4M3), scales=warm_s[:], in_=warm[:])
         ps_warm = psum_d.tile([P, NH], F32, name="ps_d")
 
         def keep_warm(passes):
@@ -259,30 +265,27 @@ def tile_clipped_task_arithmetic_s4_kernel(
                     out=ps_warm[:, 0:P], lhsT=warm_q[:].bitcast(E4M3), lhsT_scale=warm_s[:], rhs=warm_q[:].bitcast(E4M3), rhs_scale=warm_s[:], start=True, stop=True
                 )
 
-        keep_warm(WARM[0])
+        keep_warm(WARM)
         order_u(0, 0, nc.vector)
         order_u(0, 1, nc.vector)
-        turn_x(0)
-        turn_x(1)
-        keep_warm(WARM[1])
-        quantize_x(0)
         lim_cols = lim_bf[:].rearrange("p i g t -> p (i g t)")
         nc.vector.tensor_copy(out=lim_hi[:], in_=lim_cols)
         nc.vector.tensor_scalar(out=lim_lo[:], in0=lim_cols, scalar1=-1.0, scalar2=None, op0=ALU.mult)
+        order_u(1, 0, nc.vector)
+        order_u(1, 1, nc.vector)
         task_vectors(0, ONV[0])
-        turn_x(2)
-        turn_x(3)
+        for m in range(0, 4):
+            turn_x(m)
         task_vectors(1, ONV[1])
         clip_rest(0, ONV[0])
-        order_u(1, 0, nc.vector)
+        clip_rest(1, ONV[1])
+        quantize_x(0)
         interleave(0, VCS[0], VCS[0] < NH)
         quantize_x(1)
-        clip_rest(1, ONV[1])
         quantize(0)
         for m in range(4, 8):
             turn_x(m)
         interleave(1, VCS[1], VCS[1] < NH)
-        order_u(1, 1, nc.vector)
         quantize_x(2)
         quantize(1)
         quantize_x(3)

from contextlib import ExitStack

import concourse.mybir as mybir
from concourse.masks import make_identity

M, K, N, R, T = 1024, 1024, 1024, 512, 2

F32 = mybir.dt.float32
BF16 = mybir.dt.bfloat16
I32 = mybir.dt.int32
U32 = mybir.dt.uint32
U8 = mybir.dt.uint8
E4M3 = mybir.dt.float8_e4m3fn_x4
E2M1 = mybir.dt.float4_e2m1fn_x4
ALU = mybir.AluOpType
ACT = mybir.ActivationFunctionType

FLOPS = 2 * M * K * N * (1 + T) + 2 * T * R * K * N

P = 128
NH = 512
MT = M // P
G = K // 512
H = N // NH
VCS = (512, 512, 512, 256, 224, 224, 192, 128)
ONV = ((), (1, 2), (), (1, 2), (), (), (), ())
POS = 4
GCL = ()
WARM = 24
SG = ()
YS = (1, 2, 1, 2, 2, 0, 0, 0)


def tile_clipped_task_arithmetic_s4_kernel(
    tc, x, w_words, w_scales, u_words, u_scales, v_words, v_scales, lim, lam, out
):
    nc = tc.nc
    with ExitStack() as ctx:
        keep = ctx.enter_context(tc.tile_pool(name="keep", bufs=1))
        work = ctx.enter_context(tc.tile_pool(name="work", bufs=4))
        psum_d = ctx.enter_context(tc.psum_pool(name="psum_d", bufs=4))
        psum_z = ctx.enter_context(tc.psum_pool(name="psum_z", bufs=4))
        ctx.enter_context(tc.manual_schedule())

        u_raw = [keep.tile([P, 2 * K], U8, name=f"u_raw{i}", align_bytes=64) for i in range(T)]
        u_ord = [keep.tile([P, G, 4, P, 2], U8, name=f"u_ord{i}", align_bytes=64) for i in range(T)]
        us_raw = keep.tile([P, T * K], U8, name="us_raw", align_bytes=64)
        us_ord = [keep.tile([P, G, 4, P], U8, name=f"us_ord{i}", align_bytes=64) for i in range(T)]
        v_sb = [[keep.tile([P, 2 * NH], U8, name=f"v{i}_{h}", align_bytes=64) for h in range(H)] for i in range(T)]
        vs_sb = keep.tile([P, T * N], U8, name="vs_sb", align_bytes=64)
        w_sb = [keep.tile([P, N * 4], U8, name=f"w{g}", align_bytes=64) for g in range(G)]
        ws_sb = keep.tile([P, G, N], U8, name="ws_sb", align_bytes=64)
        x_sb = [keep.tile([P, 2, K], BF16, name=f"x{c}", align_bytes=64) for c in range(MT // 2)]
        xq = [keep.tile([P, 4, P], U32, name=f"xq{c}", align_bytes=64) for c in range(MT // 2)]
        xs = [keep.tile([P, 4, P], U8, name=f"xs{c}", align_bytes=64) for c in range(MT // 2)]
        cq = [keep.tile([P, NH], U32, name=f"cq{j}", align_bytes=64) for j in range(8)]
        cs = [keep.tile([P, NH], U8, name=f"cs{j}", align_bytes=64) for j in range(8)]
        acc = [[keep.tile([P, NH], F32, name=f"acc{h}_{m}", align_bytes=64) for m in range(MT)] for h in range(H)]
        warm = keep.tile([P, 4 * P], BF16, name="warm", align_bytes=64)
        warm_q = keep.tile([P, P], U32, name="warm_q", align_bytes=64)
        warm_s = keep.tile([P, P], U8, name="warm_s", align_bytes=64)
        act_dummy = keep.tile([P, 1], F32, name="act_dummy")
        ident = keep.tile([P, P], F32, name="ident")
        lim_bf = keep.tile([P, T, G, 4], BF16, name="lim_bf")
        lim_hi = keep.tile([P, T * G * 4], F32, name="lim_hi")
        lim_lo = keep.tile([P, T * G * 4], F32, name="lim_lo")
        lam_bf = keep.tile([P, MT * T], BF16, name="lam_bf")
        lam_f = keep.tile([P, MT * T], F32, name="lam_f")

        def load_u(i, eng):
            eng.dma_start(out=u_raw[i][:].bitcast(I32), in_=u_words[0, :, 2 * K * i : 2 * K * (i + 1)].bitcast(I32))

        def load_v(i, h, eng):
            c0 = 2 * (N * i + NH * h)
            eng.dma_start(out=v_sb[i][h][:].bitcast(I32), in_=v_words[0, :, c0 : c0 + 2 * NH].bitcast(I32))

        def load_scales(dst, rows, engines):
            for q in range(4):
                engines[q].dma_start(out=dst[32 * q : 32 * q + 4, :].bitcast(I32), in_=rows[4 * q : 4 * q + 4, :].bitcast(I32))

        nc.vector.memset(us_raw[:].bitcast(I32), 0)
        nc.vector.memset(vs_sb[:].bitcast(I32), 0)
        nc.vector.memset(warm[:].bitcast(I32), 0)
        x_view = x.rearrange("(p c m) k -> c p m k", c=MT // 2, m=2)

        def load_x(c):
            nc.sync.dma_start(out=x_sb[c][:], in_=x_view[c])

        def load_w(g):
            nc.sync.dma_start(out=w_sb[g][:].bitcast(I32), in_=w_words[g].rearrange("p n t -> p (n t)").bitcast(I32))

        nc.gpsimd.memset(ws_sb[:].rearrange("p g n -> p (g n)").bitcast(I32), 0)
        nc.gpsimd.dma_start(out=lim_bf[:], in_=lim.rearrange("i (g p t) -> p i g t", g=G, t=4))
        make_identity(nc, ident[:])
        load_u(0, nc.sync)
        load_v(0, 0, nc.sync)
        for q in range(4):
            nc.sync.dma_start(out=us_raw[32 * q : 32 * q + 4, :].bitcast(I32), in_=u_scales[0, 4 * q : 4 * q + 4, :].bitcast(I32))
        for q in range(4):
            nc.scalar.dma_start(out=vs_sb[32 * q : 32 * q + 4, :].bitcast(I32), in_=v_scales[0, 4 * q : 4 * q + 4, :].bitcast(I32))
        load_x(0)
        load_x(1)
        load_u(1, nc.sync)
        load_v(1, 0, nc.sync)
        load_x(2)
        load_x(3)
        for q in range(4):
            nc.sync.dma_start(
                out=ws_sb[32 * q : 32 * q + 4, :, :].bitcast(I32),
                in_=w_scales[:, 4 * q : 4 * q + 4, :].rearrange("g r n -> r g n").bitcast(I32),
            )
        load_w(0)
        load_w(1)
        nc.sync.dma_start(out=lam_bf[:], in_=lam.rearrange("(p m) i -> p (m i)", m=MT))
        load_v(0, 1, nc.sync)
        load_v(1, 1, nc.sync)

        nc.gpsimd.tensor_copy(out=lam_f[:], in_=lam_bf[:])

        units = [(h, i, g) for h in range(H) for i in range(T) for g in range(G)]

        def order_u(i, g, eng):
            eng.tensor_copy(
                out=u_ord[i][:, g, :, :, :],
                in_=u_raw[i][:, 1024 * g : 1024 * (g + 1)].rearrange("p (m t b) -> p t m b", t=4, b=2),
            )
            eng.tensor_copy(
                out=us_ord[i][:, g, :, :],
                in_=us_raw[:, K * i + 512 * g : K * i + 512 * (g + 1)].rearrange("p (m t) -> p t m", t=4),
            )

        d_sb = {}
        grp = {}

        def task_vectors(j, on_vector=(), ts=range(4)):
            h, i, g = units[j]
            if j not in d_sb:
                d_sb[j] = work.tile([P, 4, NH], BF16, name="d_sb", align_bytes=64)
            for t in ts:
                ps = psum_d.tile([P, NH], F32, name="ps_d")
                nc.tensor.matmul_mx(
                    out=ps[:],
                    lhsT=u_ord[i][:, g, t, :, :].rearrange("p m b -> p (m b)").bitcast(E2M1),
                    lhsT_scale=us_ord[i][:, g, t, :],
                    rhs=v_sb[i][h][:].bitcast(E2M1),
                    rhs_scale=vs_sb[:, N * i + NH * h : N * i + NH * (h + 1)],
                    start=True,
                    stop=True,
                )
                if t in on_vector:
                    clip(j, t, ps[:])
                else:
                    nc.scalar.copy(out=d_sb[j][:, t, :], in_=ps[:])

        def clip(j, t, src):
            h, i, g = units[j]
            c = (i * G + g) * 4 + t
            eng = nc.gpsimd if (j, t) in GCL else nc.vector
            eng.tensor_scalar(
                out=d_sb[j][:, t, :], in0=src, scalar1=lim_hi[:, c : c + 1], scalar2=lim_lo[:, c : c + 1], op0=ALU.min, op1=ALU.max
            )

        def clip_rest(j, on_vector):
            for t in range(4):
                if t not in on_vector:
                    clip(j, t, d_sb[j][:, t, :])

        def interleave(j, cols, scalar_cols):
            grp[j] = work.tile([P, NH, 4], BF16, name="grp", align_bytes=64)
            if cols > 0:
                nc.vector.tensor_copy(
                    out=grp[j][:, 0:cols, :].rearrange("p (c i) t -> p c t i", i=4), in_=d_sb[j][:, :, 0:cols].rearrange("p t (c i) -> p c t i", i=4)
                )
            if scalar_cols:
                nc.scalar.copy(
                    out=grp[j][:, cols:NH, :].rearrange("p (c i) t -> p c t i", i=4), in_=d_sb[j][:, :, cols:NH].rearrange("p t (c i) -> p c t i", i=4)
                )

        def quantize(j):
            nc.vector.quantize_mx(out=cq[j][:].bitcast(E4M3), scales=cs[j][:], in_=grp[j][:].rearrange("p n t -> p (n t)"))

        xg = {}

        def turn_x(m):
            c, mm = divmod(m, 2)
            if mm == 0:
                xg[c] = work.tile([P, 4, P, 4], BF16, name="xg", align_bytes=64)
            ps = psum_z.tile([P, G, 2, P], F32, name="ps_z")
            words = x_sb[c][:, mm, :].bitcast(F32)
            for g in range(G):
                for u in range(2):
                    nc.tensor.transpose(ps[:, g, u, :], words[:, 256 * g + u : 256 * (g + 1) : 2], ident[:])
            nc.scalar.copy(
                out=xg[c][:, 2 * mm : 2 * mm + 2, :, :].bitcast(F32),
                in_=ps[:].rearrange("p g u n -> p g n u"),
            )

        def quantize_x(c):
            nc.vector.quantize_mx(
                out=xq[c][:].rearrange("p a n -> p (a n)").bitcast(E4M3),
                scales=xs[c][:].rearrange("p a n -> p (a n)"),
                in_=xg[c][:].rearrange("p a n t -> p (a n t)"),
            )

        def x_times(m, rhs, rhs_scale, cols=slice(0, NH)):
            c, mm = divmod(m, 2)
            ps = psum_z.tile([P, NH], F32, name="ps_z")
            for g in range(G):
                nc.tensor.matmul_mx(
                    out=ps[:, cols],
                    lhsT=xq[c][:, 2 * mm + g, :].bitcast(E4M3),
                    lhsT_scale=xs[c][:, 2 * mm + g, :],
                    rhs=rhs[g][:, cols].bitcast(E4M3),
                    rhs_scale=rhs_scale[g][:, cols],
                    start=(g == 0),
                    stop=(g == G - 1),
                )
            return ps

        def base(h, m):
            ps = x_times(
                m,
                [w_sb[g][:].bitcast(U32)[:, NH * h : NH * (h + 1)] for g in range(G)],
                [ws_sb[:, g, NH * h : NH * (h + 1)] for g in range(G)],
            )
            nc.scalar.copy(out=acc[h][m][:], in_=ps[:])

        out_view = out.rearrange("(p m) n -> m p n", m=MT)

        late = []

        def task(pair, m, on_scalar=False, cols=slice(0, NH)):
            h, i = divmod(pair, T)
            ps = x_times(
                m,
                [cq[2 * pair + g] for g in range(G)],
                [cs[2 * pair + g] for g in range(G)],
                cols,
            )
            lam_col = lam_f[:, m * T + i : m * T + i + 1]
            if on_scalar:
                part = work.tile([P, NH], F32, name="part", align_bytes=64)
                nc.scalar.activation(out=part[:], in_=ps[:], func=ACT.Copy, scale=lam_col)
                nc.gpsimd.tensor_tensor(out=acc[h][m][:], in0=acc[h][m][:], in1=part[:], op=ALU.add)
            else:
                nc.vector.scalar_tensor_tensor(out=acc[h][m][:, cols], in0=ps[:, cols], scalar=lam_col, in1=acc[h][m][:, cols], op0=ALU.mult, op1=ALU.add)
            if i == T - 1:
                late.append((h, m, cols))
                if not on_scalar:
                    store(late.pop())
                    if len(late) > 0 and m - late[0][1] >= 2:
                        store(late.pop(0))

        def store(hm):
            h, m, cols = hm
            nc.sync.dma_start(out=out_view[m][:, NH * h + cols.start : NH * h + cols.stop], in_=acc[h][m][:, cols])

        nc.scalar.activation(out=act_dummy[:], in_=warm[:, 0:1], func=ACT.Copy, scale=1.0)
        nc.vector.quantize_mx(out=warm_q[:].bitcast(E4M3), scales=warm_s[:], in_=warm[:])
        ps_warm = psum_d.tile([P, NH], F32, name="ps_d")

        def keep_warm(passes):
            for r in range(passes):
                nc.tensor.matmul_mx(
                    out=ps_warm[:, 0:P], lhsT=warm_q[:].bitcast(E4M3), lhsT_scale=warm_s[:], rhs=warm_q[:].bitcast(E4M3), rhs_scale=warm_s[:], start=True, stop=True
                )

        keep_warm(WARM)
        order_u(0, 0, nc.vector)
        order_u(0, 1, nc.vector)
        lim_cols = lim_bf[:].rearrange("p i g t -> p (i g t)")
        nc.vector.tensor_copy(out=lim_hi[:], in_=lim_cols)
        nc.vector.tensor_scalar(out=lim_lo[:], in0=lim_cols, scalar1=-1.0, scalar2=None, op0=ALU.mult)
        order_u(1, 0, nc.vector)
        order_u(1, 1, nc.vector)
        task_vectors(0, ONV[0])
        for m in range(0, 4):
            turn_x(m)
        task_vectors(1, ONV[1])
        clip_rest(0, ONV[0])
        clip_rest(1, ONV[1])
        quantize_x(0)
        interleave(0, VCS[0], VCS[0] < NH)
        quantize_x(1)
        quantize(0)
        for m in range(4, 8):
            turn_x(m)
        interleave(1, VCS[1], VCS[1] < NH)
        quantize_x(2)
        quantize(1)
        quantize_x(3)
        task_vectors(2, ONV[2])
        clip_rest(2, ONV[2])
        base(0, 0)
        interleave(2, VCS[2], VCS[2] < NH)
        for m in range(1, 8):
            if m == POS:
                task_vectors(3, ONV[3])
                quantize(2)
            base(0, m)
        ym = 0
        for k in range(8):
            pair, first = divmod(k, 2)
            ms = range(4 * first, 4 * first + 4)
            j = k + 3
            if j < 8:
                clip_rest(j, ONV[j])
            task(pair, ms[0], (k, 0) in SG)
            if j + 1 < 8:
                task_vectors(j + 1, ONV[j + 1], (0, 1))
            if j < 8:
                interleave(j, VCS[j], VCS[j] < NH)
            task(pair, ms[1], (k, 1) in SG)
            if j + 1 < 8:
                task_vectors(j + 1, ONV[j + 1], (2, 3))
            task(pair, ms[2], (k, 2) in SG)
            if j < 8:
                quantize(j)
            for r in range(YS[k]):
                base(1, ym)
                ym += 1
            if k < 7:
                task(pair, ms[3], (k, 3) in SG)
            else:
                task(pair, ms[3], cols=slice(0, NH // 2))
                task(pair, ms[3], cols=slice(NH // 2, NH))
        for hm in late:
            store(hm)
